import numpy as np, ml_dtypes
CORES = [6,15,38,47]
N = 4
import mx_ref
BF = ml_dtypes.bfloat16
def gentries(a):
    return np.ascontiguousarray(a.reshape(8, 16, -1).transpose(0, 2, 1)).reshape(8, -1)
def gtable(e):
    e = np.asarray(e); return np.ascontiguousarray(e.reshape(8, -1, 16).transpose(0, 2, 1)).reshape(128, -1).astype(np.int32)
def gcols(t, e):
    v = np.concatenate([t.reshape(8, 16, -1, 4), np.zeros((8, 16, 1, 4), BF)], axis=2)
    return np.ascontiguousarray(np.stack([v[g][:, e[g]] for g in range(8)])).reshape(128, -1)
def gpick(z, e):
    return np.concatenate([z[16 * g:16 * g + 16][:, e[g]] for g in range(8)])
def tile(rs):
    return np.stack(rs, axis=2).reshape(128, -1).astype(BF)
def pick(q, e):
    c = np.concatenate([q[0].reshape(128, -1, 4), np.zeros((128, 1, 4), np.uint8)], axis=1); s = np.concatenate([q[1], np.ones((16, 1), np.uint8)], axis=1)
    return (np.ascontiguousarray(c[:, e].reshape(128, -1)), np.ascontiguousarray(s[:, e]))
def join(*qs):
    return (np.concatenate([q[0] for q in qs], axis=1), np.concatenate([q[1] for q in qs], axis=1))
def put(q, e, v):
    c, s = q[0].reshape(128, -1, 4).copy(), q[1].copy(); c[:, e] = v[0].reshape(128, -1, 4); s[:, e] = v[1]
    return (c.reshape(128, -1), s)
def pk(c, s):
    return (np.ascontiguousarray(c), mx_ref.live(s))
def emit(q):
    return q[0], q[1]
def packed(v, rng):
    q = [mx_ref.quantize(np.ascontiguousarray(v[r])) for r in range(N)]
    return np.stack([a for a, b in q]), np.stack([mx_ref.plane(b, rng) for a, b in q])
def values_of_codes():
    e, c = np.zeros((128, 128, 4), np.float32), np.zeros((128, 2, 4), np.uint8)
    e[np.arange(128), np.arange(128), 0] = 1
    c[:127, :, 0] = np.arange(256).reshape(2, 128).T[:127]
    return mx_ref.matmul(mx_ref.quantize(e.reshape(128, 512).astype(BF)), (c.reshape(128, 8), np.full((16, 2), 127, np.uint8))).T.reshape(-1).astype(np.float64)
CODE_VALUE, SCALE_VALUE = values_of_codes(), 2.0 ** (np.arange(256) - 127.0)
def decode(q):
    return (CODE_VALUE[q[0]].reshape(16, 8, -1, 4) * SCALE_VALUE[q[1]][:, None, :, None] + 0.0).reshape(128, -1).astype(np.float32)
def f(rng, *shape):
    return mx_ref.flush((rng.standard_normal(shape, dtype=np.float32) * np.exp2(rng.integers(-2, 3, shape[:-1] + (1,)))).astype(BF))
def wide(rng, *shape, cols=0):
    v = rng.standard_normal(shape, dtype=np.float32) * np.exp2(rng.integers(-12, 13, shape)).astype(np.float32)
    if cols: v *= np.repeat(np.exp2(rng.integers(-cols, cols + 1, shape[:-2] + (1, shape[-1] // 4))) * (rng.random(shape[:-2] + (1, shape[-1] // 4)) > 0.0625), 4, axis=-1).astype(np.float32)
    return mx_ref.flush(v.astype(BF))
C = 416
STEP = [1, 2, 3]
def numbers_of(rng):
    return {"x": np.array(f(rng, N, 128, 4 * C)), "u": np.array(f(rng, N, 128, 512)), "v": np.array(f(rng, N, 128, 512))}
def drawn(rng):
    e = np.tile(np.arange(C), (N, 8, 1))
    p, k, s, m = rng.permuted(e, axis=2), rng.permuted(e, axis=2), rng.permuted(e, axis=2), np.zeros_like(e)
    np.put_along_axis(m, s[:, :, ::2], s[:, :, 1::2], 2)
    np.put_along_axis(m, s[:, :, 1::2], s[:, :, ::2], 2)
    return p, k, m
def stored(p, k, m):
    return {"pg": np.stack([gtable(p[r]) for r in range(N)]), "kg": np.stack([gtable(k[r]) for r in range(N)]), "mg": np.stack([gtable(m[r]) for r in range(N)])}
def layers(rng):
    return np.array(f(rng, N, 128, 2048)).reshape(N, 8, 16, 4, 8, 16, 4)
def weights(rng, w):
    c, s = packed(np.ascontiguousarray(w).reshape(N, 128, 2048), rng)
    return {"wc": c, "ws": s}
def setup_inputs(rng):
    return {**numbers_of(rng), **stored(*drawn(rng)), **weights(rng, layers(rng))}
def setup_inputs_ties(rng):
    d = numbers_of(rng)
    o = rng.permutation(N)
    s = rng.integers(-1, 2, (N, 2, 8, C))
    s[o[0]] = 0
    s[o[1]] = 1
    s[o[2], 0] = np.where(np.arange(C) % 2 == 1, 1, rng.integers(-1, 1, (8, C)))
    x = d["x"].astype(np.float32).reshape(N, 8, 16, C, 4)
    u = d["u"].astype(np.float32).reshape(N, 128, 128, 4)
    for i in range(2):
        x[:, :, i] = 0
        x[:, :, i, :, 0] = s[:, i]
        u[:, :, i::16] = 0
        for h in range(0, 128, 16): u[:, h + i, h + i, 0] = 1
    p, k, m = drawn(rng)
    p[o[2]] = k[o[2]] = np.arange(C)
    m[o[2]] = np.arange(C) ^ 1
    w = layers(rng)
    w[:, :, :, :, :, :8] = 0
    return {"x": x.reshape(N, 128, 4 * C).astype(BF), "u": u.reshape(N, 128, 512).astype(BF), "v": d["v"], **stored(p, k, m), **weights(rng, w)}
def setup_inputs_near(rng):
    d = numbers_of(rng)
    o = rng.permutation(N)
    k = np.where(o % 2 == 0, 2.0 ** -30, 1.0)
    x = np.zeros((N, 8, 16, C, 4))
    s = rng.integers(-1, 2, (N, 2, 8, C)) * k[:, None, None, None]
    for i in range(2):
        x[:, :, 2 * i, :, 0] = 1.125 * s[:, i]
        x[:, :, 2 * i + 1, :, 0] = -1.25 * s[:, i]
    x[:, :, 9, :, 0] = rng.choice([-1.0, 1.0], (N, 8, C)) * 2.0 ** -17
    x[:, :, 10:] = rng.choice([-1.0, 1.0], (N, 8, 6, C, 4)) * (1 + 0.125 * rng.integers(0, 8, (N, 8, 6, C, 4))) * np.exp2(-12.0 - rng.integers(0, 4, (N, 8, 6, C, 4)))
    u = d["u"].astype(np.float32).reshape(N, 128, 128, 4)
    u[:, :, ::16] = 0
    u[:, :, 1::16] = 0
    w = layers(rng)
    w[:, :, :8] = 0
    w[:, :, :, :, :, :10] = 0
    for r in range(N):
        for g in rng.permutation(8)[:4]: x[r, g, 0, rng.integers(C), 0] = 2.0 ** 30 * rng.choice([-1.0, 1.0])
        if o[r] == 0:
            x[r, :, :8] = 0
            x[r, :, 0, :, 0] = 2.0 ** -30
        for g in range(8):
            h = 16 * g
            if o[r] == 0:
                u[r, h + 4, h, 0] = 2.0 ** -30
                u[r, h + 4, h + 1, 0] = -2.0 ** -30
                w[r, g, 8, 0, g, 4, 0] = 2.0 ** -8
                w[r, g, 9, 0, g, 4, 0] = 2.0 ** -22
            else:
                for i in range(2):
                    u[r, h + 2 * i, h + i, 0] = 1.125 * k[r]
                    u[r, h + 2 * i + 1, h + i, 0] = k[r]
    return {"x": x.astype(np.float32).reshape(N, 128, 4 * C).astype(BF), "u": u.reshape(N, 128, 512).astype(BF), "v": d["v"], **stored(*drawn(rng)), **weights(rng, w)}
def setup_inputs_odd(rng):
    d = numbers_of(rng)
    x = (1.0 + (2 * rng.integers(0, 64, (N, 16, 8, C, 4)) + 1) * 2.0 ** -7) * np.exp2(-rng.integers(0, 7, (N, 16, 8, C, 4)).astype(np.float64)) * rng.choice([-1.0, 1.0], (N, 16, 8, C, 4))
    x[:, ::2, 0, :, 0] = 1.96875 * 2.0 ** 8 * rng.choice([-1.0, 1.0], (8, 1))
    x[:, 1::2, 0, :, 0] = 1.96875 * 2.0 ** 8 * rng.choice([-1.0, 1.0], (N, 8, C))
    u = d["u"].astype(np.float32).reshape(N, 16, 8, 128, 4)
    u[:, :, 0, ::16] = 0
    u[:, :, :, 1::16] = 0
    h = rng.permutation(8) % 4
    for g in range(8):
        x[:, 2 * g, 1, :, 0] = (8 + rng.integers(0, 2, (N, C))) * 2.0 ** (int(h[g]) - 9)
        x[:, 2 * g, 2, :, 0] = -2.0 ** (int(h[g]) - 6)
        u[:, 2 * g, 1:3, 16 * g + 1, 0] = 1
    w = layers(rng)
    for i in (0, 8):
        w[:, :, i] = 0
        w[:, :, :, :, :, i] = 0
    w[:, :, :, 0, :, 1:3] = 0
    for g in range(8): w[:, g, 0, 0, g, 0, 0] = -0.5
    p, k, m = drawn(rng)
    t = int(rng.integers(N))
    p[t] = m[t] = np.arange(C)
    k[t] = rng.permutation(C)
    return {"x": x.astype(np.float32).reshape(N, 128, 4 * C).astype(BF), "u": u.reshape(N, 128, 512).astype(BF), "v": d["v"], **stored(p, k, m), **weights(rng, w)}
def setup_inputs_ends(rng):
    d = numbers_of(rng)
    o, ep, ek, em = [rng.permutation(N) % 4 for i in range(4)]
    s = rng.choice([-1.0, 1.0], (N, 128, C, 4))
    s[o == 0] = -1
    s[o == 1] = rng.choice([-1.0, 1.0], (N, 1, C, 1))[o == 1]
    x = s * (0.90 + 0.02 * rng.random((N, 128, C, 4))) * 2.0 ** 30
    tiny = (1 + 0.125 * rng.integers(0, 8, (N, 128, C, 4))) * 2.0 ** -30
    x[o == 3] = (s * tiny)[o == 3]
    x[:, 8:16] = tiny[:, 8:16]
    u = d["u"].astype(np.float32).reshape(N, 128, 128, 4)
    for r in range(N):
        h = rng.permutation(8)
        size = 2.0 ** -30 if o[r] == 3 else 2.0 ** 30
        u[r, :, ::16] = ((h % 2 * 2 - 1) * size)[None, :, None]
        u[r, :, 1::16] = ((h // 2 % 2 * 2 - 1) * size)[None, :, None]
    v = rng.choice([-1.0, 1.0], (N, 128, 512)) * np.where(o % 2 == 0, 2.0 ** 30, 2.0 ** -30)[:, None, None]
    p, k, m = drawn(rng)
    line = np.arange(C)
    p[ep == 0] = line
    p[ep == 1] = (line + 1) % C
    p[ep == 2] = C - 1 - line
    k[ek == 0] = line
    k[ek == 1] = C - 1 - line
    k[ek == 2] = (line + C - 1) % C
    m[em == 0] = line
    m[em == 1] = C - 1 - line
    m[em == 2] = line ^ 1
    w = np.zeros((N, 128, 4, 128, 4), np.float32)
    i = np.arange(128)
    for b in range(4): w[:, i, b, i, b] = np.where((i >= 8) & (i < 16), np.where(o == 3, 2.0 ** 8, 2.0 ** -8)[:, None], -0.25)
    return {"x": x.astype(np.float32).reshape(N, 128, 4 * C).astype(BF), "u": u.reshape(N, 128, 512).astype(BF), "v": v.astype(np.float32).astype(BF), **stored(p, k, m), **weights(rng, w.astype(BF))}
def setup_inputs_spread(rng):
    d = setup_inputs(rng)
    d["x"] = wide(rng, N, 128, 4 * C, cols=6)
    return d
def check_inputs(d):
    b = []
    for k in ("x", "u", "v"):
        a = np.abs(d[k].astype(np.float32))
        if not (np.isfinite(a).all() and ((a == 0) | (a >= 2.0 ** -30) & (a <= 2.0 ** 30)).all()): b.append("a value of " + k)
    none, least, most = [emit(mx_ref.quantize(np.full((128, 16), k, np.float32).astype(BF)))[1][0, 0] for k in (0.0, 2.0 ** -8, 2.0 ** 8)]
    top = emit(mx_ref.quantize(np.full((128, 16), 1.9921875, np.float32).astype(BF)))[0][0, 0] & 0x7F
    line = np.arange(C)
    for r in range(N):
        for k in ("pg", "kg"):
            if not (np.sort(gentries(d[k][r]), axis=1) == line).all(): b.append(k + ": no permutation")
        m = gentries(d["mg"][r])
        if not ((m >= 0) & (m < C)).all(): b.append("an entry of mg")
        elif not (np.take_along_axis(m, m, 1) == line).all(): b.append("mg: a mate's mate")
        if ((d["wc"][r] == 0x7F) | (d["wc"][r] == 0xFF)).any(): b.append("wc: a code that is no number")
        if ((d["wc"][r] & 0x7F) > top).any(): b.append("wc: a code that quantize_mx does not give")
        s = mx_ref.live(d["ws"][r])
        if ((s != none) & ((s < least) | (s > most))).any(): b.append("ws: a scale out of range")
    return b
def reference(x, u, v, pg, kg, mg, wc, ws):
    qu = [mx_ref.quantize(u[r]) for r in range(N)]
    lay = [pk(wc[r], ws[r]) for r in range(N)]
    p, k, m = [[gentries(a[r]).astype(np.int64) for r in range(N)] for a in (pg, kg, mg)]
    now = [x[r] for r in range(N)]
    for step in STEP:
        own, land, mosaic = [], [], []
        for r in range(N):
            q = mx_ref.quantize(now[r])
            s = mx_ref.matmul(qu[r], q)
            first = (s[::16] > 0).astype(np.int64)
            e = first + 2 * (s[1::16] > 0).astype(np.int64)
            at = np.zeros((8, C), np.int64)
            for g in range(8):
                power = np.ones(C, np.int64) if g == 0 else e[g - 1][at[g - 1]]
                a = k[r][g]
                for i in range(3): a = np.where(i < power, p[r][g][a], a)
                at[g] = a
            bit = np.take_along_axis(first, at, 1)
            p[r] = np.where(bit != np.take_along_axis(bit, m[r], 1), np.take_along_axis(p[r], m[r], 1), p[r])
            land.append(at)
            own.append(decode(q))
            mosaic.append(mx_ref.quantize(gcols(own[r].astype(BF), at)))
        made = []
        for r in range(N):
            h = [mx_ref.matmul(pick(lay[r], np.arange(128 * b, 128 * b + 128)), mosaic[r ^ step]) * np.float32(0.03125) for b in range(4)]
            made.append(tile([own[r][:, b::4] + gpick(h[b], land[r]) for b in range(4)]))
        now = made
    y, pl = np.zeros((N, 128, C), np.float32), np.zeros((N, 8, 2 * C), np.float32)
    oc, osc = np.zeros((N, 128, 4 * C), np.uint8), np.zeros((N, 16, C), np.uint8)
    for r in range(N):
        q = mx_ref.quantize(now[r])
        y[r] = mx_ref.matmul(mx_ref.quantize(v[r]), q)
        pl[r] = np.concatenate([land[r], p[r]], axis=1)
        oc[r], osc[r] = emit(q)
    return {"y": y, "pl": pl, "oc": oc, "osc": osc}

@@ -1,0 +1,503 @@
+from concourse.bass import DstId, RemoteDMATransfer
+from concourse.mybir import dt, AluOpType, ActivationFunctionType
+
+C = 416
+CA = 224
+NL = C // 16
+STEP = (1, 2, 3)
+F32, BF16, I32, U16, CODE, U8 = "float32", "bfloat16", "int32", "uint16", "float8_e4m3fn_x4", "uint8"
+
+SCRATCH, PART = {}, {}
+
+
+def _buf(cols, dtype, *names, where="sbuf"):
+    for name in names:
+        SCRATCH[name] = (where, [128, cols], dtype)
+
+
+def _parts(whole, cols, dtype, *names):
+    SCRATCH[whole] = ("sbuf", [128, cols * len(names)], dtype)
+    for i, name in enumerate(names):
+        PART[name] = (whole, i * cols, cols)
+
+
+_buf(512, F32, *["pb%d" % i for i in range(8)], where="psum")
+_buf(2, I32, "ip")
+_buf(12, I32, "ib")
+_buf(16, F32, "cols", "d00")
+_buf(520, F32, "i520")
+_buf(512, F32, "icg", "i3")
+_buf(C, F32, "jm", "kk", "kt", "yt")
+_buf(C, BF16, "kb", "bw", "scw", "z", "zz", "nd", "ns")
+_buf(64, F32, "im")
+_buf(64, BF16, "maska")
+_buf(128, F32, "thr")
+_buf(NL, I32, "iw", "kgw", "mgw")
+_buf(8, I32, "iu")
+_buf(8, U16, "lu0", "lu1")
+_buf(4, U16, "la4")
+_buf(2, U16, "lrep")
+_buf(520, BF16, "w1")
+_buf(560, BF16, "w2")
+_buf(512, BF16, "pat", "msk", "w3", "ut", "vt", "at")
+_buf(NL, F32, "jw", "mf", "mj", "t0", "td", "nm", "tau")
+_buf(NL, U16, "lpos", "lm", "ltau")
+_buf(C, I32, "pgf")
+_buf(4 * C, BF16, "xt", "x2", "x3", "x4", "zt")
+_buf(2048, BF16, "mt")
+for _c, _s, _n in (("uq", "uqs", 128), ("vq", "vqs", 128), ("wq", "wqs", 512), ("b3", "b3s", 128), ("mq", "mqs", 512), ("aq", "aqs", 128), ("zq", "zqs", C)):
+    _buf(_n, CODE, _c)
+    _buf(_n, U8, _s)
+_parts("upc", 128, CODE, "up", "uc")
+_parts("upp", 128, U8, "ups", "ucs")
+_parts("ec", 128, CODE, *["e%d" % i for i in range(4)])
+_parts("ep", 128, U8, *["es%d" % i for i in range(4)])
+_parts("bc", 128, CODE, *["b2%d" % i for i in range(4)])
+_parts("bp", 128, U8, *["b2s%d" % i for i in range(4)])
+_parts("hs", C, F32, *["hs%d" % i for i in range(4)])
+_parts("fb", C, BF16, *["fb%d" % i for i in range(4)])
+_parts("fp", C, BF16, *["fp%d" % i for i in range(4)])
+_parts("tg", C, F32, "tg1", "tg2", "tg3")
+_parts("tsum", C, F32, "ts1", "ts2", "ts3")
+_parts("tf", NL, F32, "tf1", "tf2", "tf3")
+_parts("lists", NL, U16, "l0", "l1", "l2", "l3")
+_buf(112, F32, "sc", "d0")
+_buf(4 * NL, F32, "ph", "sl", "cs1", "cs2", "cs3")
+_buf(2 * C, F32, "pl_t")
+for _i in (1, 2, 3, 4):
+    _buf(C, CODE, "qc%d" % _i)
+    _buf(C, U8, "qs%d" % _i)
+for _i in (1, 2, 3):
+    _buf(C, F32, "p%d" % _i)
+    _buf(C, CODE, "rc%d" % _i)
+    _buf(C, U8, "rs%d" % _i)
+    _buf(NL, U16, "la%d" % _i, "lp%d" % _i)
+
+SEMAPHORES = ["s_v", "s_a", "s_p", "s_g", "loc"] + ["d_%d" % i for i in range(40)] + ["r_%s%d" % (k, i) for k in "csl" for i in (1, 2, 3)]
+
+WAKE = 100.0
+CY = 0.83
+
+
+def _hit(a, b):
+    if a[1] >= b[2] or b[1] >= a[2]:
+        return False
+    if a[3] == b[3] and a[3] > 1:
+        return a[1] % a[3] == b[1] % a[3]
+    return True
+
+
+def rank_program(g, core, T, topo):
+    rank = T.rank_of(core)
+    if rank is None:
+        return
+    A = AluOpType
+    AF = ActivationFunctionType
+    ops, seen = [], {}
+
+    def V(name, lo=0, hi=None, st=1):
+        whole, at, cols = PART.get(name, (name, 0, SCRATCH.get(name, (0, (0, 0)))[1][1]))
+        return (whole, at + lo, at + (cols if hi is None else hi), st)
+
+    def ap(v):
+        return T[v[0]][:, v[1]:v[2]] if v[3] == 1 else T[v[0]][:, v[1]:v[2]:v[3]]
+
+    def ind(v, l):
+        return ap(v).indirect(ap(l))
+
+    def n_of(v):
+        return -(-(v[2] - v[1]) // v[3])
+
+    def add(q, cost, reads, writes, emit, kind="c", sem=None, amount=0, after=()):
+        i = len(ops)
+        deps = {}
+        for mode, views in ((0, reads), (1, writes)):
+            for v in views:
+                if v is None:
+                    continue
+                psum = v[0].startswith("pb")
+                for (j, m, w) in seen.setdefault(v[0], []):
+                    if j == i:
+                        continue
+                    same = ops[j]["q"] == q and len(q) == 1
+                    if psum:
+                        if same and not (m or mode):
+                            continue
+                    elif not (m or mode) or not _hit(v, w):
+                        continue
+                    raw = m == 1 and mode == 0
+                    deps[j] = deps.get(j, False) or raw
+                seen[v[0]].append((i, mode, v))
+        for j in after:
+            deps[j] = True
+        ops.append({"q": q, "cost": cost, "deps": deps, "emit": emit, "kind": kind, "sem": sem, "amount": amount})
+        return i
+
+    def vcost(n, f=1.0):
+        return max(64.0, n * f) * CY
+
+    def gcost(n):
+        return 50 + 1.3 * n * CY
+
+    def ts(out, in0, s1, s2, op0, op1=None, q="V", f=1.0, lst=None):
+        rd = [in0, lst] + [s for s in (s1, s2) if isinstance(s, tuple)]
+        def emit(e):
+            a1 = ap(s1) if isinstance(s1, tuple) else s1
+            a2 = ap(s2) if isinstance(s2, tuple) else s2
+            src = ap(in0) if lst is None else ind(in0, lst)
+            if op1 is None:
+                return e.tensor_scalar(ap(out), src, a1, None, op0)
+            return e.tensor_scalar(ap(out), src, a1, a2, op0, op1)
+        return add(q, vcost(n_of(out), f) if lst is None else gcost(n_of(out)), rd, [out], emit)
+
+    def tt(out, in0, in1, op, lst=None, f=1.0):
+        def emit(e):
+            return e.tensor_tensor(ap(out), ap(in0) if lst is None else ind(in0, lst), ap(in1), op)
+        return add("V", vcost(n_of(out), f) if lst is None else gcost(n_of(out)), [in0, in1, lst], [out], emit)
+
+    def copy(out, in_):
+        return add("V", vcost(n_of(out)), [in_], [out], lambda e: e.tensor_copy(ap(out), ap(in_)))
+
+    def fill(out, val):
+        return add("V", vcost(n_of(out), 0.5), [], [out], lambda e: e.memset(ap(out), val))
+
+    def scan(out, d0, d1, f=1.0):
+        return add("V", vcost(n_of(out), f), [d0, d1], [out], lambda e: e.tensor_tensor_scan(ap(out), ap(d0), ap(d1), 0.0, A.mult, A.add))
+
+    def act(out, in_, func, lst=None, scale=None):
+        def emit(e):
+            src = ap(in_) if lst is None else ind(in_, lst)
+            if scale is None:
+                return e.activation(ap(out), src, func)
+            return e.activation(ap(out), src, func, scale=scale)
+        return add("A", vcost(n_of(out)) if lst is None else 15 + gcost(n_of(out)), [in_, lst], [out], emit)
+
+    def either(out, in_, lst, relu=False):
+        def emit(e, eng):
+            if eng == "V":
+                if relu:
+                    return e.tensor_scalar(ap(out), ind(in_, lst), 0.0, None, A.max)
+                return e.tensor_copy(ap(out), ind(in_, lst))
+            return e.activation(ap(out), ind(in_, lst), AF.Relu if relu else AF.Copy)
+        return add("VA", gcost(n_of(out)), [in_, lst], [out], emit)
+
+    def out_of_psum(out, in_, scale=None, q="A"):
+        def emit(e, eng=None):
+            if eng == "V" or q == "V":
+                if scale is None:
+                    return e.tensor_copy(ap(out), ap(in_))
+                return e.tensor_scalar(ap(out), ap(in_), scale, None, A.mult)
+            if scale is None:
+                return e.activation(ap(out), ap(in_), AF.Copy)
+            return e.activation(ap(out), ap(in_), AF.Copy, scale=scale)
+        return add(q, vcost(n_of(out)), [in_], [out], emit)
+
+    def quant(c, s, t):
+        return add("V", 12 + 0.22 * n_of(t), [t], [c, s], lambda e: e.quantize_mx(ap(c), ap(s), ap(t)))
+
+    def mm(out, terms, after=()):
+        def emit(e):
+            last = None
+            for k, (a, b, c, d) in enumerate(terms):
+                last = e.matmul_mx(ap(out), ap(a), ap(b), ap(c), ap(d), k == 0, k == len(terms) - 1)
+            return last
+        return add("P", (n_of(out) + 16) * CY * 1.3 * len(terms), [v for t in terms for v in t], [out], emit, after=after)
+
+    def iota(out, pattern, base, cm):
+        small = SCRATCH[out[0]][2] == F32
+        def emit(e):
+            if small:
+                return e.iota(ap(out), pattern, base, cm, allow_small_or_imprecise_dtypes=True)
+            return e.iota(ap(out), pattern, base, cm)
+        return add("G", 130 + 2 * n_of(out) * CY, [], [out], emit)
+
+    dcount = [0]
+
+    def dma(q, reads, writes, pairs, cost=2000.0):
+        sem = "d_%d" % dcount[0]
+        dcount[0] += 1
+        def emit(e):
+            for o, i in pairs():
+                e.dma_start(o, i).then_inc(T.sem[sem], 16)
+            return None
+        return add(q, cost, reads, writes, emit, "d", sem, 16 * len(pairs()))
+
+    def send(r, what, dst_v, src_v, codes, latency):
+        to = T.cores[rank ^ STEP[r - 1]]
+        rid, pid = topo.addr(to)[0], topo.addr(to)[1]
+        mask, k = topo.mask(core, to), len(topo.engines(core, to))
+        sem = "r_%s%d" % (what, r)
+        def emit(e):
+            o, i = (ap(dst_v).bitcast(dt.uint8), ap(src_v).bitcast(dt.uint8)) if codes else (ap(dst_v), ap(src_v))
+            e.remote_dma(o, i, T.sem[sem], T.sem["loc"], pid, rid, mask)
+            sent[0] += k
+            return None
+        j = add("G", 150.0, [src_v], [], emit, "s")
+        add("R", latency, [], [dst_v], None, "r", sem, k, after=(j,))
+
+    sent = [0]
+    col = lambda i: V("cols", i, i + 1)
+    QC, HC, P4, Q1, SP, G0, THQ, SCQ, R4 = [col(i) for i in range(9)]
+
+    dma("S", [], [V("pgf")], lambda: [(T["pgf"][i::16, :], T.pg[:, :]) for i in range(0, 16, 2)], 2500.0)
+    dma("A", [], [V("pgf"), V("kgw")], lambda: [(T["kgw"][:, :], T.kg[:, :])] + [(T["pgf"][i::16, :], T.pg[:, :]) for i in range(1, 16, 2)], 2500.0)
+    ops[-1]["deps"] = {}
+    dma("S", [], [V("ut")], lambda: [(T["ut"][:, :], T.u[:, :])], 2800.0)
+    dma("S", [], [V("xt", 0, 4 * CA)], lambda: [(T["xt"][:, 0:4 * CA], T.x[:, 0:4 * CA])], 3000.0)
+    dma("S", [], [V("xt", 4 * CA)], lambda: [(T["xt"][:, 4 * CA:4 * C], T.x[:, 4 * CA:4 * C])], 3000.0)
+    dma("S", [], [V("mgw")], lambda: [(T["mgw"][:, :], T.mg[:, :])])
+    dma("S", [], [V("wq")], lambda: [(T["wq"][:, :].bitcast(dt.uint8), T.wc[:, :])], 3000.0)
+    dma("S", [], [V("wqs")], lambda: [(T["wqs"][:, :], T.ws[:, :])])
+    dma("S", [], [V("vt")], lambda: [(T["vt"][:, :], T.v[:, :])])
+
+    ipv = V("ip", 0, 1)
+    iota(ipv, [[0, 1]], 0, 1)
+    iota(V("iw"), [[1, NL]], 0, 0)
+    iota(V("iu"), [[16, 8]], 0, 0)
+    ib = lambda i: V("ib", i, i + 1)
+    ts(ib(0), ipv, 15, None, A.bitwise_and)
+    ts(ib(1), ipv, 4, None, A.logical_shift_right)
+    ts(ib(2), ipv, 3, None, A.bitwise_and)
+    ts(ib(3), ipv, 12, None, A.bitwise_and)
+    ts(ib(4), ipv, 8, 3, A.bitwise_and, A.logical_shift_right)
+    copy(QC, ib(0))
+    copy(HC, ib(1))
+    ts(R4, ib(2), 4, 3, A.mult, A.add)
+    copy(col(9), ib(4))
+    ts(col(10), QC, float(NL), None, A.mult)
+    ts(V("lpos"), V("iw"), col(10), None, A.add)
+    copy(V("l0"), V("kgw"))
+    iota(V("jm"), [[0, NL], [1, 16]], 0, 0)
+    ts(Q1, QC, 1.0, None, A.add)
+    ts(V("kt"), V("jm"), Q1, 16383.0, A.is_equal, A.mult)
+    ts(V("kk"), V("jm"), QC, None, A.not_equal)
+    kk2 = V("jm")
+    tt(kk2, V("kk"), V("kt"), A.add, f=2.0)
+    ts(col(11), QC, 15.0, 2.0 ** -14 - 1.0, A.is_lt, A.mult)
+    ts(SCQ, col(11), 1.0, None, A.add)
+    ts(V("lu1"), V("iu"), col(9), None, A.add)
+    copy(V("lu0"), V("iu"))
+    quant(V("uq"), V("uqs"), V("ut"))
+    for c, s, l in (("up", "ups", "lu1"), ("uc", "ucs", "lu0")):
+        add("V", gcost(128), [V("uq"), V(l)], [V(c)], lambda e, c=c, l=l: e.tensor_copy(ap(V(c)).bitcast(dt.uint32), ap(V("uq")).bitcast(dt.uint32).indirect(ap(V(l)))))
+        add("A", 15 + gcost(128), [V("uqs"), V(l)], [V(s)], lambda e, s=s, l=l: e.activation(ap(V(s)), ap(V("uqs")).indirect(ap(V(l))), AF.Copy))
+    add("V", gcost(C), [V("pgf"), V("lpos")], [V("p1")], lambda e: e.tensor_copy(ap(V("p1")), ind(V("pgf"), V("lpos"))))
+    copy(V("t0"), V("kgw"))
+
+    def powers(r):
+        before = V("t0")
+        for n in (1, 2, 3):
+            tg, tsv, ln, tf = V("tg%d" % n), V("ts%d" % n), V("l%d" % n), V("tf%d" % n)
+            act(tg, V("p%d" % r), AF.Copy, lst=V("l%d" % (n - 1)))
+            scan(tsv, kk2, tg)
+            ts(ln, V("ts%d" % n, 15, C, 16), SCQ, None, A.mult)
+            copy(tf, ln)
+            d = V("cs%d" % r, 3 - n, 4 * NL, 4)
+            tt(d, tf, before, A.subtract)
+            if n == 1:
+                ts(V("td"), d, G0, None, A.mult)
+                tt(V("cs%d" % r, 3, 4 * NL, 4), V("td"), before, A.add)
+            before = tf
+
+    ts(G0, ipv, 16, None, A.is_lt)
+    powers(1)
+    iota(V("i520"), [[1, 520]], 0, 0)
+    ts(P4, ipv, 4, 4, A.mult, A.add)
+    ts(V("w1"), V("i520"), P4, None, A.is_equal)
+    for b in range(4):
+        quant(V("e%d" % b), V("es%d" % b), V("w1", 4 - b, 516 - b))
+    iota(V("icg"), [[1, 8], [0, 64]], 0, 0)
+    ts(col(12), QC, 8.0, 2.0, A.is_equal, A.mult)
+    ts(col(13), QC, 0.0, None, A.is_equal)
+    tt(SP, col(12), col(13), A.add)
+    fill(V("pat"), 0.0)
+    for o, val in ((3, 1.0), (6, 1.0), (9, 1.0), (12, 1.0), (2, -1.0), (5, -1.0), (8, -1.0)):
+        fill(V("pat", o, 512, 64), val)
+    ts(V("msk"), V("icg"), HC, SP, A.is_equal, A.mult)
+    fill(V("w2", 0, 48), 0.0)
+    tt(V("w2", 48, 560), V("msk"), V("pat"), A.mult, f=2.0)
+    for c in range(4):
+        quant(V("b2%d" % c), V("b2s%d" % c), V("w2", 48 - 16 * c, 560 - 16 * c))
+    iota(V("i3"), [[1, 32], [0, 4], [-8, 4]], 0, 0)
+    ts(V("w3"), V("i3"), HC, None, A.is_equal)
+    quant(V("b3"), V("b3s"), V("w3"))
+    iota(V("im"), [[1, 16], [0, 4]], 0, 0)
+    ts(V("maska"), V("im"), QC, None, A.is_equal)
+    for i, val in enumerate((100.0, 3.0, 2.0, 1.0)):
+        fill(V("thr", i, 128, 4), val)
+    fill(V("d00"), 0.0)
+    fill(V("d00", 3, 16, 4), 1.0)
+    ts(V("lrep", 0, 1), ib(3), 3.0, None, A.add)
+    fill(V("im", 0, 4), 0.0)
+    ts(V("la4"), V("im", 0, 4), R4, None, A.add)
+    fill(V("at", 0, 64), 0.0)
+    fill(V("mt", 1536, 2048), 0.0)
+    quant(V("mq", 384), V("mqs", 384), V("mt", 1536, 2048))
+    ts(col(14), QC, 15.0, 2.0 ** -20 - 1.0, A.is_lt, A.mult)
+    ts(THQ, col(14), 1.0, None, A.add)
+    ts(V("kb"), V("kt"), 64.0, None, A.mult)
+    tt(V("kb"), V("kb"), V("kk"), A.add)
+    copy(V("lm"), V("mgw"))
+    copy(V("mf"), V("mgw"))
+    ts(V("jw"), V("iw"), 16.0, QC, A.mult, A.add)
+    tt(V("mj"), V("mf"), V("jw"), A.subtract)
+    ts(V("mj"), V("mj"), THQ, None, A.mult)
+    ts(V("jw"), V("jw"), 0.25, None, A.add)
+
+    def state(r, x, rows=(("up", "ups"),)):
+        for i, (a, b) in enumerate(((0, CA), (CA, C))):
+            quant(V("qc%d" % r, a, b), V("qs%d" % r, a, b), V(x, 4 * a, 4 * b))
+            mm(V("pb%d" % i, 0, b - a), [(V(rows[0][0]), V(rows[0][1]), V("qc%d" % r, a, b), V("qs%d" % r, a, b))])
+
+    for r in (1, 2, 3):
+        x = ("xt", "x2", "x3")[r - 1]
+        qc, qs, la, lp = V("qc%d" % r), V("qs%d" % r), V("la%d" % r), V("lp%d" % r)
+        state(r, x)
+        send(r, "c", V("rc%d" % r), qc, True, 6000.0)
+        send(r, "s", V("rs%d" % r), qs, False, 4000.0)
+        act(V("bw", 0, CA), V("pb0", 0, CA), AF.Sign)
+        act(V("bw", CA, C), V("pb1", 0, C - CA), AF.Sign)
+        for n in range(4):
+            either(V("mt", n, 4 * C, 4), V("bw"), V("l%d" % n), relu=True)
+        quant(V("mq", 0, C), V("mqs", 0, C), V("mt", 0, 4 * C))
+        mm(V("pb6", 0, 128), [(V("mq", 128 * c, 128 * c + 128), V("mqs", 128 * c, 128 * c + 128), V("b2%d" % c), V("b2s%d" % c)) for c in range(4)])
+        first = len(ops) - 1
+        for k in range(7):
+            sck = V("sc", 16 * k, 16 * k + 16)
+            scan(sck, V("d0", 16 * k, 16 * k + 16) if k else V("d00"), V("pb6", 16 * k, 16 * k + 16))
+            if k < 6:
+                tt(V("d0", 16 * k + 16, 16 * k + 32), sck, V("thr", 0, 16), A.is_ge, lst=V("lrep", 0, 1))
+            tt(V("at", 64 * k + 64, 64 * k + 128), sck, V("maska"), A.mult, lst=V("la4"))
+        quant(V("aq"), V("aqs"), V("at"))
+        mm(V("pb7", 0, 128), [(V("aq"), V("aqs"), V("b3"), V("b3s"))])
+        tt(V("ph"), V("pb7", 0, 104), V("thr", 0, 104), A.is_ge)
+        scan(V("sl"), V("ph"), V("cs%d" % r))
+        copy(la, V("sl", 3, 104, 4))
+        send(r, "l", lp, la, False, 2200.0)
+        for b in range(4):
+            mm(V("pb%d" % (2 + b), 0, C), [(V("e%d" % b), V("es%d" % b), qc, qs)], after=(first,))
+            out_of_psum(V("fb%d" % b), V("pb%d" % (2 + b), 0, C))
+        mm(V("pb0", 0, C), [(V("uc"), V("ucs"), qc, qs)])
+        act(V("scw"), V("pb0", 0, C), AF.Sign)
+        for b in range(4):
+            mm(V("pb%d" % (2 + b), 0, C), [(V("e%d" % b), V("es%d" % b), V("rc%d" % r), V("rs%d" % r))])
+            out_of_psum(V("fp%d" % b), V("pb%d" % (2 + b), 0, C))
+        act(V("z"), V("scw"), AF.Relu, lst=la)
+        ts(V("zz"), V("scw"), 0.0, None, A.max, lst=la)
+        tt(V("nd"), V("z"), V("zz"), A.not_equal, lst=V("lm"))
+        scan(V("ns"), V("kb"), V("nd"), f=0.5)
+        tt(V("nm"), V("ns", 15, C, 16), V("mj"), A.mult)
+        tt(V("tau"), V("nm"), V("jw"), A.add)
+        copy(V("ltau"), V("tau"))
+        act(V("p%d" % (r + 1)) if r < 3 else V("pl_t", C, 2 * C), V("p%d" % r), AF.Copy, lst=V("ltau"))
+        if r == 3:
+            act(V("pl_t", 0, C), V("i520", 0, C), AF.Copy, lst=la)
+            dma("S", [V("pl_t")], [], lambda: [(T.pl[:, :], T["pl_t"][0::16, :])])
+        for t in range(4):
+            either(V("zt", t, 4 * C, 4), V("fp%d" % t), lp)
+        quant(V("zq"), V("zqs"), V("zt"))
+        for b in range(4):
+            mm(V("pb%d" % (2 + b), 0, C), [(V("wq", 128 * b, 128 * b + 128), V("wqs", 128 * b, 128 * b + 128), V("zq"), V("zqs"))])
+            out_of_psum(V("hs%d" % b), V("pb%d" % (2 + b), 0, C), scale=0.03125)
+        nx = ("x2", "x3", "x4")[r - 1]
+        for a, e in ((0, CA), (CA, C)):
+            for b in range(4):
+                tt(V(nx, 4 * a + b, 4 * e, 4), V("hs%d" % b), V("fb%d" % b, a, e), A.add, lst=V("la%d" % r, a // 16, e // 16))
+        if r < 3:
+            powers(r + 1)
+    quant(V("vq"), V("vqs"), V("vt"))
+    for i, (a, b) in enumerate(((0, CA), (CA, C))):
+        quant(V("qc4", a, b), V("qs4", a, b), V("x4", 4 * a, 4 * b))
+        dma("S", [V("qc4", a, b)], [], lambda a=a, b=b: [(T.oc[:, 4 * a:4 * b], T["qc4"][:, a:b].bitcast(dt.uint8))])
+        mm(V("pb%d" % i, 0, b - a), [(V("vq"), V("vqs"), V("qc4", a, b), V("qs4", a, b))])
+        out_of_psum(V("yt", a, b), V("pb%d" % i, 0, b - a))
+        dma("S", [V("yt", a, b)], [], lambda a=a, b=b: [(T.y[:, a:b], T["yt"][:, a:b])])
+    dma("S", [V("qs4")], [], lambda: [(T.osc[4 * k:4 * k + 4, :], T["qs4"][32 * k:32 * k + 4, :]) for k in range(4)])
+
+    n = len(ops)
+    users = [[] for _ in range(n)]
+    for i, o in enumerate(ops):
+        for j in o["deps"]:
+            users[j].append(i)
+    prio = [0.0] * n
+    for i in range(n - 1, -1, -1):
+        prio[i] = ops[i]["cost"] + max([prio[u] + WAKE for u in users[i]] + [0.0])
+    free = {k: 0.0 for k in "VAPGSR"}
+    end = [None] * n
+    left = [len(o["deps"]) for o in ops]
+    ready = [i for i in range(n) if not left[i]]
+    order = []
+    while ready:
+        best = None
+        cand = []
+        for i in ready:
+            o = ops[i]
+            at = max([end[j] + WAKE for j in o["deps"]] + [0.0])
+            if o["kind"] == "r":
+                at = end[list(o["deps"])[0]] if len(o["deps"]) == 1 else max(end[j] for j in o["deps"])
+                cand.append((at, i, "R"))
+                continue
+            for q in o["q"]:
+                cand.append((max(at, free[q]), i, q))
+        first = min(c[0] for c in cand)
+        best = max((c for c in cand if c[0] <= first + 20.0), key=lambda c: (prio[c[1]], -c[0]))
+        at, i, q = best
+        o = ops[i]
+        if o["kind"] == "d":
+            free[q] = at + 60.0 * (o["amount"] // 16)
+            end[i] = free[q] + o["cost"]
+        elif o["kind"] == "r":
+            end[i] = at + o["cost"]
+        else:
+            free[q] = end[i] = at + o["cost"]
+        order.append((i, q, at))
+        ready.remove(i)
+        for u in users[i]:
+            left[u] -= 1
+            if not left[u]:
+                ready.append(u)
+
+    eng = {"V": g.vector, "A": g.scalar, "P": g.tensor, "G": g, "S": g.sync}
+    csem = {"V": "s_v", "A": "s_a", "P": "s_p", "G": "s_g"}
+    count = {k: 0 for k in csem}
+    known = {k: {} for k in "VAPGS"}
+    token, clock, qof = [None] * n, [None] * n, [None] * n
+    for i, q, at in order:
+        o = ops[i]
+        qof[i] = q
+        if o["kind"] == "r":
+            token[i], clock[i] = (o["sem"], o["amount"]), {o["sem"]: o["amount"]}
+            for j in o["deps"]:
+                for s, v in (clock[j] or {}).items():
+                    clock[i][s] = max(clock[i].get(s, 0), 0)
+            continue
+        e = eng[q]
+        need = []
+        for j, raw in o["deps"].items():
+            if token[j] is None:
+                continue
+            need.append(j)
+        need.sort(key=lambda j: -end[j])
+        for j in need:
+            s, v = token[j]
+            if known[q].get(s, 0) >= v:
+                continue
+            e.wait_ge(T.sem[s], v)
+            for s2, v2 in clock[j].items():
+                known[q][s2] = max(known[q].get(s2, 0), v2)
+        call = o["emit"](e, q) if len(o["q"]) > 1 else o["emit"](e)
+        if o["kind"] == "c":
+            count[q] += 1
+            call.then_inc(T.sem[csem[q]], 1)
+            token[i] = (csem[q], count[q])
+        elif o["kind"] == "d":
+            token[i] = (o["sem"], o["amount"])
+        if token[i]:
+            clock[i] = dict(known[q])
+            clock[i][token[i][0]] = max(clock[i].get(token[i][0], 0), token[i][1])
+    for q in csem:
+        g.wait_ge(T.sem[csem[q]], count[q])
+    for o in ops:
+        if o["kind"] in "dr":
+            g.wait_ge(T.sem[o["sem"]], o["amount"])
+    g.wait_ge(T.sem["loc"], sent[0])

@@ -26,22 +26,22 @@ _buf(2, I32, "ip")
 _buf(12, I32, "ib")
 _buf(16, F32, "cols", "d00")
 _buf(520, F32, "i520")
-_buf(512, F32, "icg", "i3")
-_buf(C, F32, "jm", "kk", "kt", "yt")
+_buf(C, F32, "kk", "yt")
+_buf(16, F32, "j16", "k16", "n16", "t16")
 _buf(C, BF16, "kb", "bw", "scw", "z", "zz", "nd", "ns")
 _buf(64, F32, "im")
 _buf(64, BF16, "maska")
 _buf(128, F32, "thr")
-_buf(NL, I32, "iw", "kgw", "mgw")
+_buf(NL, I32, "iw", "kgw", "mgw", "pgw")
 _buf(8, I32, "iu")
 _buf(8, U16, "lu0", "lu1")
 _buf(4, U16, "la4")
 _buf(2, U16, "lrep")
-_buf(520, BF16, "w1")
+_buf(520, BF16, "w1", "ones")
 _buf(560, BF16, "w2")
-_buf(512, BF16, "pat", "msk", "w3", "ut", "vt", "at")
+_buf(512, BF16, "pat", "msk", "msk2", "w3", "w3a", "ut", "vt", "at")
 _buf(NL, F32, "jw", "mf", "mj", "t0", "td", "nm", "tau")
-_buf(NL, U16, "lpos", "lm", "ltau")
+_buf(NL, U16, "lpos", "lm", "ltau", "lpw", "lq")
 _buf(C, I32, "pgf")
 _buf(4 * C, BF16, "xt", "x2", "x3", "x4", "zt")
 _buf(2048, BF16, "mt")
@@ -76,6 +76,8 @@ for _i in (1, 2, 3):
 SEMAPHORES = ["s_v", "s_a", "s_p", "s_g", "loc"] + ["d_%d" % i for i in range(40)] + ["r_%s%d" % (k, i) for k in "csl" for i in (1, 2, 3)]
 
 WAKE = 100.0
+LOOK = 0.0
+BIAS = 300.0
 CY = 0.83
 
 
@@ -93,7 +95,7 @@ def rank_program(g, core, T, topo):
         return
     A = AluOpType
     AF = ActivationFunctionType
-    ops, seen = [], {}
+    ops, seen, bias = [], {}, [0.0]
 
     def V(name, lo=0, hi=None, st=1):
         whole, at, cols = PART.get(name, (name, 0, SCRATCH.get(name, (0, (0, 0)))[1][1]))
@@ -130,7 +132,7 @@ def rank_program(g, core, T, topo):
                 seen[v[0]].append((i, mode, v))
         for j in after:
             deps[j] = True
-        ops.append({"q": q, "cost": cost, "deps": deps, "emit": emit, "kind": kind, "sem": sem, "amount": amount})
+        ops.append({"q": q, "cost": cost, "deps": deps, "emit": emit, "kind": kind, "sem": sem, "amount": amount, "bias": bias[0]})
         return i
 
     def vcost(n, f=1.0):
@@ -169,8 +171,8 @@ def rank_program(g, core, T, topo):
             src = ap(in_) if lst is None else ind(in_, lst)
             if scale is None:
                 return e.activation(ap(out), src, func)
-            return e.activation(ap(out), src, func, scale=scale)
-        return add("A", vcost(n_of(out)) if lst is None else 15 + gcost(n_of(out)), [in_, lst], [out], emit)
+            return e.activation(ap(out), src, func, scale=ap(scale))
+        return add("A", vcost(n_of(out)) if lst is None else 15 + gcost(n_of(out)), [in_, lst, scale], [out], emit)
 
     def either(out, in_, lst, relu=False):
         def emit(e, eng):
@@ -211,6 +213,9 @@ def rank_program(g, core, T, topo):
             return e.iota(ap(out), pattern, base, cm)
         return add("G", 130 + 2 * n_of(out) * CY, [], [out], emit)
 
+    def keep(out, in_, pattern, op, base, cm):
+        return add("G", 170 + 2 * n_of(out) * CY, [in_], [out], lambda e: e.affine_select(ap(out), ap(in_), pattern, op, 0.0, base, cm))
+
     dcount = [0]
 
     def dma(q, reads, writes, pairs, cost=2000.0):
@@ -242,9 +247,10 @@ def rank_program(g, core, T, topo):
     dma("S", [], [V("pgf")], lambda: [(T["pgf"][i::16, :], T.pg[:, :]) for i in range(0, 16, 2)], 2500.0)
     dma("A", [], [V("pgf"), V("kgw")], lambda: [(T["kgw"][:, :], T.kg[:, :])] + [(T["pgf"][i::16, :], T.pg[:, :]) for i in range(1, 16, 2)], 2500.0)
     ops[-1]["deps"] = {}
+    dma("A", [], [V("pgw")], lambda: [(T["pgw"][:, :], T.pg[:, :])])
     dma("S", [], [V("ut")], lambda: [(T["ut"][:, :], T.u[:, :])], 2800.0)
     dma("S", [], [V("xt", 0, 4 * CA)], lambda: [(T["xt"][:, 0:4 * CA], T.x[:, 0:4 * CA])], 3000.0)
-    dma("S", [], [V("xt", 4 * CA)], lambda: [(T["xt"][:, 4 * CA:4 * C], T.x[:, 4 * CA:4 * C])], 3000.0)
+    dma("A", [], [V("xt", 4 * CA)], lambda: [(T["xt"][:, 4 * CA:4 * C], T.x[:, 4 * CA:4 * C])], 3000.0)
     dma("S", [], [V("mgw")], lambda: [(T["mgw"][:, :], T.mg[:, :])])
     dma("S", [], [V("wq")], lambda: [(T["wq"][:, :].bitcast(dt.uint8), T.wc[:, :])], 3000.0)
     dma("S", [], [V("wqs")], lambda: [(T["wqs"][:, :], T.ws[:, :])])
@@ -267,12 +273,16 @@ def rank_program(g, core, T, topo):
     ts(col(10), QC, float(NL), None, A.mult)
     ts(V("lpos"), V("iw"), col(10), None, A.add)
     copy(V("l0"), V("kgw"))
-    iota(V("jm"), [[0, NL], [1, 16]], 0, 0)
+    iota(V("j16"), [[1, 16]], 0, 0)
+    copy(V("lpw"), V("pgw"))
     ts(Q1, QC, 1.0, None, A.add)
-    ts(V("kt"), V("jm"), Q1, 16383.0, A.is_equal, A.mult)
-    ts(V("kk"), V("jm"), QC, None, A.not_equal)
-    kk2 = V("jm")
-    tt(kk2, V("kk"), V("kt"), A.add, f=2.0)
+    ts(V("t16"), V("j16"), Q1, 16383.0, A.is_equal, A.mult)
+    ts(V("n16"), V("j16"), QC, None, A.not_equal)
+    tt(V("k16"), V("n16"), V("t16"), A.add)
+    fill(V("tau"), 0.0)
+    ts(V("lq"), V("tau"), QC, None, A.add)
+    kk2 = V("kk")
+    act(kk2, V("k16"), AF.Copy, lst=V("lq"))
     ts(col(11), QC, 15.0, 2.0 ** -14 - 1.0, A.is_lt, A.mult)
     ts(SCQ, col(11), 1.0, None, A.add)
     ts(V("lu1"), V("iu"), col(9), None, A.add)
@@ -280,7 +290,7 @@ def rank_program(g, core, T, topo):
     quant(V("uq"), V("uqs"), V("ut"))
     for c, s, l in (("up", "ups", "lu1"), ("uc", "ucs", "lu0")):
         add("V", gcost(128), [V("uq"), V(l)], [V(c)], lambda e, c=c, l=l: e.tensor_copy(ap(V(c)).bitcast(dt.uint32), ap(V("uq")).bitcast(dt.uint32).indirect(ap(V(l)))))
-        add("A", 15 + gcost(128), [V("uqs"), V(l)], [V(s)], lambda e, s=s, l=l: e.activation(ap(V(s)), ap(V("uqs")).indirect(ap(V(l))), AF.Copy))
+        add("V", gcost(128), [V("uqs"), V(l)], [V(s)], lambda e, s=s, l=l: e.tensor_copy(ap(V(s)), ap(V("uqs")).indirect(ap(V(l)))))
     add("V", gcost(C), [V("pgf"), V("lpos")], [V("p1")], lambda e: e.tensor_copy(ap(V("p1")), ind(V("pgf"), V("lpos"))))
     copy(V("t0"), V("kgw"))
 
@@ -288,7 +298,12 @@ def rank_program(g, core, T, topo):
         before = V("t0")
         for n in (1, 2, 3):
             tg, tsv, ln, tf = V("tg%d" % n), V("ts%d" % n), V("l%d" % n), V("tf%d" % n)
-            act(tg, V("p%d" % r), AF.Copy, lst=V("l%d" % (n - 1)))
+            if r == 1:
+                if n > 1:
+                    either(V("p%d" % n), V("p%d" % (n - 1)), V("lpw"))
+                either(tg, V("p%d" % n), V("l0"))
+            else:
+                act(tg, V("p%d" % r), AF.Copy, lst=V("l%d" % (n - 1)))
             scan(tsv, kk2, tg)
             ts(ln, V("ts%d" % n, 15, C, 16), SCQ, None, A.mult)
             copy(tf, ln)
@@ -301,25 +316,24 @@ def rank_program(g, core, T, topo):
 
     ts(G0, ipv, 16, None, A.is_lt)
     powers(1)
-    iota(V("i520"), [[1, 520]], 0, 0)
-    ts(P4, ipv, 4, 4, A.mult, A.add)
-    ts(V("w1"), V("i520"), P4, None, A.is_equal)
+    fill(V("ones"), 1.0)
+    keep(V("w1"), V("ones"), [[1, 520]], A.is_equal, -4, -4)
     for b in range(4):
         quant(V("e%d" % b), V("es%d" % b), V("w1", 4 - b, 516 - b))
-    iota(V("icg"), [[1, 8], [0, 64]], 0, 0)
     ts(col(12), QC, 8.0, 2.0, A.is_equal, A.mult)
     ts(col(13), QC, 0.0, None, A.is_equal)
     tt(SP, col(12), col(13), A.add)
     fill(V("pat"), 0.0)
     for o, val in ((3, 1.0), (6, 1.0), (9, 1.0), (12, 1.0), (2, -1.0), (5, -1.0), (8, -1.0)):
         fill(V("pat", o, 512, 64), val)
-    ts(V("msk"), V("icg"), HC, SP, A.is_equal, A.mult)
+    keep(V("msk"), V("pat"), [[-16, 8], [0, 64]], A.is_ge, 0, 1)
+    keep(V("msk2"), V("msk"), [[16, 8], [0, 64]], A.is_ge, 15, -1)
     fill(V("w2", 0, 48), 0.0)
-    tt(V("w2", 48, 560), V("msk"), V("pat"), A.mult, f=2.0)
+    act(V("w2", 48, 560), V("msk2"), AF.Copy, scale=SP)
     for c in range(4):
         quant(V("b2%d" % c), V("b2s%d" % c), V("w2", 48 - 16 * c, 560 - 16 * c))
-    iota(V("i3"), [[1, 32], [0, 4], [-8, 4]], 0, 0)
-    ts(V("w3"), V("i3"), HC, None, A.is_equal)
+    keep(V("w3a"), V("ones", 0, 512), [[-16, 32], [0, 4], [128, 4]], A.is_ge, 0, 1)
+    keep(V("w3"), V("w3a"), [[16, 32], [0, 4], [-128, 4]], A.is_ge, 15, -1)
     quant(V("b3"), V("b3s"), V("w3"))
     iota(V("im"), [[1, 16], [0, 4]], 0, 0)
     ts(V("maska"), V("im"), QC, None, A.is_equal)
@@ -335,8 +349,9 @@ def rank_program(g, core, T, topo):
     quant(V("mq", 384), V("mqs", 384), V("mt", 1536, 2048))
     ts(col(14), QC, 15.0, 2.0 ** -20 - 1.0, A.is_lt, A.mult)
     ts(THQ, col(14), 1.0, None, A.add)
-    ts(V("kb"), V("kt"), 64.0, None, A.mult)
-    tt(V("kb"), V("kb"), V("kk"), A.add)
+    ts(V("t16"), V("t16"), 64.0, None, A.mult)
+    tt(V("n16"), V("t16"), V("n16"), A.add)
+    act(V("kb"), V("n16"), AF.Copy, lst=V("lq"))
     copy(V("lm"), V("mgw"))
     copy(V("mf"), V("mgw"))
     ts(V("jw"), V("iw"), 16.0, QC, A.mult, A.add)
@@ -391,18 +406,25 @@ def rank_program(g, core, T, topo):
         copy(V("ltau"), V("tau"))
         act(V("p%d" % (r + 1)) if r < 3 else V("pl_t", C, 2 * C), V("p%d" % r), AF.Copy, lst=V("ltau"))
         if r == 3:
+            iota(V("i520"), [[1, 520]], 0, 0)
             act(V("pl_t", 0, C), V("i520", 0, C), AF.Copy, lst=la)
             dma("S", [V("pl_t")], [], lambda: [(T.pl[:, :], T["pl_t"][0::16, :])])
-        for t in range(4):
-            either(V("zt", t, 4 * C, 4), V("fp%d" % t), lp)
-        quant(V("zq"), V("zqs"), V("zt"))
+        for a, e in ((0, CA), (CA, C)):
+            for t in range(4):
+                either(V("zt", 4 * a + t, 4 * e, 4), V("fp%d" % t), V("lp%d" % r, a // 16, e // 16))
+            quant(V("zq", a, e), V("zqs", a, e), V("zt", 4 * a, 4 * e))
         for b in range(4):
-            mm(V("pb%d" % (2 + b), 0, C), [(V("wq", 128 * b, 128 * b + 128), V("wqs", 128 * b, 128 * b + 128), V("zq"), V("zqs"))])
-            out_of_psum(V("hs%d" % b), V("pb%d" % (2 + b), 0, C), scale=0.03125)
+            bias[0] = BIAS * (3 - b)
+            for i, (a, e) in enumerate(((0, CA), (CA, C))):
+                bank = V("pb%d" % ((2, 3, 4, 5, 0, 1, 6, 7)[4 * i + b]), 0, e - a)
+                mm(bank, [(V("wq", 128 * b, 128 * b + 128), V("wqs", 128 * b, 128 * b + 128), V("zq", a, e), V("zqs", a, e))])
+                out_of_psum(V("hs%d" % b, a, e), bank, scale=0.03125)
         nx = ("x2", "x3", "x4")[r - 1]
         for a, e in ((0, CA), (CA, C)):
             for b in range(4):
+                bias[0] = BIAS * (3 - b)
                 tt(V(nx, 4 * a + b, 4 * e, 4), V("hs%d" % b), V("fb%d" % b, a, e), A.add, lst=V("la%d" % r, a // 16, e // 16))
+        bias[0] = 0.0
         if r < 3:
             powers(r + 1)
     quant(V("vq"), V("vqs"), V("vt"))
@@ -422,6 +444,7 @@ def rank_program(g, core, T, topo):
     prio = [0.0] * n
     for i in range(n - 1, -1, -1):
         prio[i] = ops[i]["cost"] + max([prio[u] + WAKE for u in users[i]] + [0.0])
+    prio = [p + o["bias"] for p, o in zip(prio, ops)]
     free = {k: 0.0 for k in "VAPGSR"}
     end = [None] * n
     left = [len(o["deps"]) for o in ops]
@@ -441,6 +464,10 @@ def rank_program(g, core, T, topo):
                 cand.append((max(at, free[q]), i, q))
         first = min(c[0] for c in cand)
         best = max((c for c in cand if c[0] <= first + 20.0), key=lambda c: (prio[c[1]], -c[0]))
+        late = best[0] + ops[best[1]]["cost"]
+        soon = [c for c in cand if c[2] == best[2] and prio[c[1]] > prio[best[1]] and c[0] - best[0] < LOOK * (late - c[0])]
+        if soon:
+            best = max(soon, key=lambda c: (prio[c[1]], -c[0]))
         at, i, q = best
         o = ops[i]
         if o["kind"] == "d":

from concourse.bass import DstId, RemoteDMATransfer
from concourse.mybir import dt, AluOpType, ActivationFunctionType

C = 416
CA = 224
NL = C // 16
STEP = (1, 2, 3)
F32, BF16, I32, U16, CODE, U8 = "float32", "bfloat16", "int32", "uint16", "float8_e4m3fn_x4", "uint8"

SCRATCH, PART = {}, {}


def _buf(cols, dtype, *names, where="sbuf"):
    for name in names:
        SCRATCH[name] = (where, [128, cols], dtype)


def _parts(whole, cols, dtype, *names):
    SCRATCH[whole] = ("sbuf", [128, cols * len(names)], dtype)
    for i, name in enumerate(names):
        PART[name] = (whole, i * cols, cols)


_buf(512, F32, *["pb%d" % i for i in range(8)], where="psum")
_buf(2, I32, "ip")
_buf(12, I32, "ib")
_buf(16, F32, "cols", "d00")
_buf(520, F32, "i520")
_buf(C, F32, "kk", "yt")
_buf(16, F32, "j16", "k16", "n16", "t16")
_buf(C, BF16, "kb", "bw", "scw", "z", "zz", "nd", "ns")
_buf(64, F32, "im")
_buf(64, BF16, "maska")
_buf(128, F32, "thr")
_buf(NL, I32, "iw", "kgw", "mgw", "pgw")
_buf(8, I32, "iu")
_buf(8, U16, "lu0", "lu1")
_buf(4, U16, "la4")
_buf(2, U16, "lrep")
_buf(520, BF16, "w1", "ones")
_buf(560, BF16, "w2")
_buf(512, BF16, "pat", "msk", "msk2", "w3", "w3a", "ut", "vt", "at")
_buf(NL, F32, "jw", "mf", "mj", "t0", "td", "nm", "tau")
_buf(NL, U16, "lpos", "lm", "ltau", "lpw", "lq")
_buf(C, I32, "pgf")
_buf(4 * C, BF16, "xt", "x2", "x3", "x4", "zt")
_buf(2048, BF16, "mt")
for _c, _s, _n in (("uq", "uqs", 128), ("vq", "vqs", 128), ("wq", "wqs", 512), ("b3", "b3s", 128), ("mq", "mqs", 512), ("aq", "aqs", 128), ("zq", "zqs", C)):
    _buf(_n, CODE, _c)
    _buf(_n, U8, _s)
_parts("upc", 128, CODE, "up", "uc")
_parts("upp", 128, U8, "ups", "ucs")
_parts("ec", 128, CODE, *["e%d" % i for i in range(4)])
_parts("ep", 128, U8, *["es%d" % i for i in range(4)])
_parts("bc", 128, CODE, *["b2%d" % i for i in range(4)])
_parts("bp", 128, U8, *["b2s%d" % i for i in range(4)])
_parts("hs", C, F32, *["hs%d" % i for i in range(4)])
_parts("fb", C, BF16, *["fb%d" % i for i in range(4)])
_parts("fp", C, BF16, *["fp%d" % i for i in range(4)])
_parts("tg", C, F32, "tg1", "tg2", "tg3")
_parts("tsum", C, F32, "ts1", "ts2", "ts3")
_parts("tf", NL, F32, "tf1", "tf2", "tf3")
_parts("lists", NL, U16, "l0", "l1", "l2", "l3")
_buf(112, F32, "sc", "d0")
_buf(4 * NL, F32, "ph", "sl", "cs1", "cs2", "cs3")
_buf(2 * C, F32, "pl_t")
for _i in (1, 2, 3, 4):
    _buf(C, CODE, "qc%d" % _i)
    _buf(C, U8, "qs%d" % _i)
for _i in (1, 2, 3):
    _buf(C, F32, "p%d" % _i)
    _buf(C, CODE, "rc%d" % _i)
    _buf(C, U8, "rs%d" % _i)
    _buf(NL, U16, "la%d" % _i, "lp%d" % _i)

SEMAPHORES = ["s_v", "s_a", "s_p", "s_g", "loc"] + ["d_%d" % i for i in range(40)] + ["r_%s%d" % (k, i) for k in "csl" for i in (1, 2, 3)]

WAKE = 100.0
LOOK = 0.0
BIAS = 300.0
CY = 0.83


def _hit(a, b):
    if a[1] >= b[2] or b[1] >= a[2]:
        return False
    if a[3] == b[3] and a[3] > 1:
        return a[1] % a[3] == b[1] % a[3]
    return True


def rank_program(g, core, T, topo):
    rank = T.rank_of(core)
    if rank is None:
        return
    A = AluOpType
    AF = ActivationFunctionType
    ops, seen, bias = [], {}, [0.0]

    def V(name, lo=0, hi=None, st=1):
        whole, at, cols = PART.get(name, (name, 0, SCRATCH.get(name, (0, (0, 0)))[1][1]))
        return (whole, at + lo, at + (cols if hi is None else hi), st)

    def ap(v):
        return T[v[0]][:, v[1]:v[2]] if v[3] == 1 else T[v[0]][:, v[1]:v[2]:v[3]]

    def ind(v, l):
        return ap(v).indirect(ap(l))

    def n_of(v):
        return -(-(v[2] - v[1]) // v[3])

    def add(q, cost, reads, writes, emit, kind="c", sem=None, amount=0, after=()):
        i = len(ops)
        deps = {}
        for mode, views in ((0, reads), (1, writes)):
            for v in views:
                if v is None:
                    continue
                psum = v[0].startswith("pb")
                for (j, m, w) in seen.setdefault(v[0], []):
                    if j == i:
                        continue
                    same = ops[j]["q"] == q and len(q) == 1
                    if psum:
                        if same and not (m or mode):
                            continue
                    elif not (m or mode) or not _hit(v, w):
                        continue
                    raw = m == 1 and mode == 0
                    deps[j] = deps.get(j, False) or raw
                seen[v[0]].append((i, mode, v))
        for j in after:
            deps[j] = True
        ops.append({"q": q, "cost": cost, "deps": deps, "emit": emit, "kind": kind, "sem": sem, "amount": amount, "bias": bias[0]})
        return i

    def vcost(n, f=1.0):
        return max(64.0, n * f) * CY

    def gcost(n):
        return 50 + 1.3 * n * CY

    def ts(out, in0, s1, s2, op0, op1=None, q="V", f=1.0, lst=None):
        rd = [in0, lst] + [s for s in (s1, s2) if isinstance(s, tuple)]
        def emit(e):
            a1 = ap(s1) if isinstance(s1, tuple) else s1
            a2 = ap(s2) if isinstance(s2, tuple) else s2
            src = ap(in0) if lst is None else ind(in0, lst)
            if op1 is None:
                return e.tensor_scalar(ap(out), src, a1, None, op0)
            return e.tensor_scalar(ap(out), src, a1, a2, op0, op1)
        return add(q, vcost(n_of(out), f) if lst is None else gcost(n_of(out)), rd, [out], emit)

    def tt(out, in0, in1, op, lst=None, f=1.0):
        def emit(e):
            return e.tensor_tensor(ap(out), ap(in0) if lst is None else ind(in0, lst), ap(in1), op)
        return add("V", vcost(n_of(out), f) if lst is None else gcost(n_of(out)), [in0, in1, lst], [out], emit)

    def copy(out, in_):
        return add("V", vcost(n_of(out)), [in_], [out], lambda e: e.tensor_copy(ap(out), ap(in_)))

    def fill(out, val):
        return add("V", vcost(n_of(out), 0.5), [], [out], lambda e: e.memset(ap(out), val))

    def scan(out, d0, d1, f=1.0):
        return add("V", vcost(n_of(out), f), [d0, d1], [out], lambda e: e.tensor_tensor_scan(ap(out), ap(d0), ap(d1), 0.0, A.mult, A.add))

    def act(out, in_, func, lst=None, scale=None):
        def emit(e):
            src = ap(in_) if lst is None else ind(in_, lst)
            if scale is None:
                return e.activation(ap(out), src, func)
            return e.activation(ap(out), src, func, scale=ap(scale))
        return add("A", vcost(n_of(out)) if lst is None else 15 + gcost(n_of(out)), [in_, lst, scale], [out], emit)

    def either(out, in_, lst, relu=False):
        def emit(e, eng):
            if eng == "V":
                if relu:
                    return e.tensor_scalar(ap(out), ind(in_, lst), 0.0, None, A.max)
                return e.tensor_copy(ap(out), ind(in_, lst))
            return e.activation(ap(out), ind(in_, lst), AF.Relu if relu else AF.Copy)
        return add("VA", gcost(n_of(out)), [in_, lst], [out], emit)

    def out_of_psum(out, in_, scale=None, q="A"):
        def emit(e, eng=None):
            if eng == "V" or q == "V":
                if scale is None:
                    return e.tensor_copy(ap(out), ap(in_))
                return e.tensor_scalar(ap(out), ap(in_), scale, None, A.mult)
            if scale is None:
                return e.activation(ap(out), ap(in_), AF.Copy)
            return e.activation(ap(out), ap(in_), AF.Copy, scale=scale)
        return add(q, vcost(n_of(out)), [in_], [out], emit)

    def quant(c, s, t):
        return add("V", 12 + 0.22 * n_of(t), [t], [c, s], lambda e: e.quantize_mx(ap(c), ap(s), ap(t)))

    def mm(out, terms, after=()):
        def emit(e):
            last = None
            for k, (a, b, c, d) in enumerate(terms):
                last = e.matmul_mx(ap(out), ap(a), ap(b), ap(c), ap(d), k == 0, k == len(terms) - 1)
            return last
        return add("P", (n_of(out) + 16) * CY * 1.3 * len(terms), [v for t in terms for v in t], [out], emit, after=after)

    def iota(out, pattern, base, cm):
        small = SCRATCH[out[0]][2] == F32
        def emit(e):
            if small:
                return e.iota(ap(out), pattern, base, cm, allow_small_or_imprecise_dtypes=True)
            return e.iota(ap(out), pattern, base, cm)
        return add("G", 130 + 2 * n_of(out) * CY, [], [out], emit)

    def keep(out, in_, pattern, op, base, cm):
        return add("G", 170 + 2 * n_of(out) * CY, [in_], [out], lambda e: e.affine_select(ap(out), ap(in_), pattern, op, 0.0, base, cm))

    dcount = [0]

    def dma(q, reads, writes, pairs, cost=2000.0):
        sem = "d_%d" % dcount[0]
        dcount[0] += 1
        def emit(e):
            for o, i in pairs():
                e.dma_start(o, i).then_inc(T.sem[sem], 16)
            return None
        return add(q, cost, reads, writes, emit, "d", sem, 16 * len(pairs()))

    def send(r, what, dst_v, src_v, codes, latency):
        to = T.cores[rank ^ STEP[r - 1]]
        rid, pid = topo.addr(to)[0], topo.addr(to)[1]
        mask, k = topo.mask(core, to), len(topo.engines(core, to))
        sem = "r_%s%d" % (what, r)
        def emit(e):
            o, i = (ap(dst_v).bitcast(dt.uint8), ap(src_v).bitcast(dt.uint8)) if codes else (ap(dst_v), ap(src_v))
            e.remote_dma(o, i, T.sem[sem], T.sem["loc"], pid, rid, mask)
            sent[0] += k
            return None
        j = add("G", 150.0, [src_v], [], emit, "s")
        add("R", latency, [], [dst_v], None, "r", sem, k, after=(j,))

    sent = [0]
    col = lambda i: V("cols", i, i + 1)
    QC, HC, P4, Q1, SP, G0, THQ, SCQ, R4 = [col(i) for i in range(9)]

    dma("S", [], [V("pgf")], lambda: [(T["pgf"][i::16, :], T.pg[:, :]) for i in range(0, 16, 2)], 2500.0)
    dma("A", [], [V("pgf"), V("kgw")], lambda: [(T["kgw"][:, :], T.kg[:, :])] + [(T["pgf"][i::16, :], T.pg[:, :]) for i in range(1, 16, 2)], 2500.0)
    ops[-1]["deps"] = {}
    dma("A", [], [V("pgw")], lambda: [(T["pgw"][:, :], T.pg[:, :])])
    dma("S", [], [V("ut")], lambda: [(T["ut"][:, :], T.u[:, :])], 2800.0)
    dma("S", [], [V("xt", 0, 4 * CA)], lambda: [(T["xt"][:, 0:4 * CA], T.x[:, 0:4 * CA])], 3000.0)
    dma("A", [], [V("xt", 4 * CA)], lambda: [(T["xt"][:, 4 * CA:4 * C], T.x[:, 4 * CA:4 * C])], 3000.0)
    dma("S", [], [V("mgw")], lambda: [(T["mgw"][:, :], T.mg[:, :])])
    dma("S", [], [V("wq")], lambda: [(T["wq"][:, :].bitcast(dt.uint8), T.wc[:, :])], 3000.0)
    dma("S", [], [V("wqs")], lambda: [(T["wqs"][:, :], T.ws[:, :])])
    dma("S", [], [V("vt")], lambda: [(T["vt"][:, :], T.v[:, :])])

    ipv = V("ip", 0, 1)
    iota(ipv, [[0, 1]], 0, 1)
    iota(V("iw"), [[1, NL]], 0, 0)
    iota(V("iu"), [[16, 8]], 0, 0)
    ib = lambda i: V("ib", i, i + 1)
    ts(ib(0), ipv, 15, None, A.bitwise_and)
    ts(ib(1), ipv, 4, None, A.logical_shift_right)
    ts(ib(2), ipv, 3, None, A.bitwise_and)
    ts(ib(3), ipv, 12, None, A.bitwise_and)
    ts(ib(4), ipv, 8, 3, A.bitwise_and, A.logical_shift_right)
    copy(QC, ib(0))
    copy(HC, ib(1))
    ts(R4, ib(2), 4, 3, A.mult, A.add)
    copy(col(9), ib(4))
    ts(col(10), QC, float(NL), None, A.mult)
    ts(V("lpos"), V("iw"), col(10), None, A.add)
    copy(V("l0"), V("kgw"))
    iota(V("j16"), [[1, 16]], 0, 0)
    copy(V("lpw"), V("pgw"))
    ts(Q1, QC, 1.0, None, A.add)
    ts(V("t16"), V("j16"), Q1, 16383.0, A.is_equal, A.mult)
    ts(V("n16"), V("j16"), QC, None, A.not_equal)
    tt(V("k16"), V("n16"), V("t16"), A.add)
    fill(V("tau"), 0.0)
    ts(V("lq"), V("tau"), QC, None, A.add)
    kk2 = V("kk")
    act(kk2, V("k16"), AF.Copy, lst=V("lq"))
    ts(col(11), QC, 15.0, 2.0 ** -14 - 1.0, A.is_lt, A.mult)
    ts(SCQ, col(11), 1.0, None, A.add)
    ts(V("lu1"), V("iu"), col(9), None, A.add)
    copy(V("lu0"), V("iu"))
    quant(V("uq"), V("uqs"), V("ut"))
    for c, s, l in (("up", "ups", "lu1"), ("uc", "ucs", "lu0")):
        add("V", gcost(128), [V("uq"), V(l)], [V(c)], lambda e, c=c, l=l: e.tensor_copy(ap(V(c)).bitcast(dt.uint32), ap(V("uq")).bitcast(dt.uint32).indirect(ap(V(l)))))
        add("V", gcost(128), [V("uqs"), V(l)], [V(s)], lambda e, s=s, l=l: e.tensor_copy(ap(V(s)), ap(V("uqs")).indirect(ap(V(l)))))
    add("V", gcost(C), [V("pgf"), V("lpos")], [V("p1")], lambda e: e.tensor_copy(ap(V("p1")), ind(V("pgf"), V("lpos"))))
    copy(V("t0"), V("kgw"))

    def powers(r):
        before = V("t0")
        for n in (1, 2, 3):
            tg, tsv, ln, tf = V("tg%d" % n), V("ts%d" % n), V("l%d" % n), V("tf%d" % n)
            if r == 1:
                if n > 1:
                    either(V("p%d" % n), V("p%d" % (n - 1)), V("lpw"))
                either(tg, V("p%d" % n), V("l0"))
            else:
                act(tg, V("p%d" % r), AF.Copy, lst=V("l%d" % (n - 1)))
            scan(tsv, kk2, tg)
            ts(ln, V("ts%d" % n, 15, C, 16), SCQ, None, A.mult)
            copy(tf, ln)
            d = V("cs%d" % r, 3 - n, 4 * NL, 4)
            tt(d, tf, before, A.subtract)
            if n == 1:
                ts(V("td"), d, G0, None, A.mult)
                tt(V("cs%d" % r, 3, 4 * NL, 4), V("td"), before, A.add)
            before = tf

    ts(G0, ipv, 16, None, A.is_lt)
    powers(1)
    fill(V("ones"), 1.0)
    keep(V("w1"), V("ones"), [[1, 520]], A.is_equal, -4, -4)
    for b in range(4):
        quant(V("e%d" % b), V("es%d" % b), V("w1", 4 - b, 516 - b))
    ts(col(12), QC, 8.0, 2.0, A.is_equal, A.mult)
    ts(col(13), QC, 0.0, None, A.is_equal)
    tt(SP, col(12), col(13), A.add)
    fill(V("pat"), 0.0)
    for o, val in ((3, 1.0), (6, 1.0), (9, 1.0), (12, 1.0), (2, -1.0), (5, -1.0), (8, -1.0)):
        fill(V("pat", o, 512, 64), val)
    keep(V("msk"), V("pat"), [[-16, 8], [0, 64]], A.is_ge, 0, 1)
    keep(V("msk2"), V("msk"), [[16, 8], [0, 64]], A.is_ge, 15, -1)
    fill(V("w2", 0, 48), 0.0)
    act(V("w2", 48, 560), V("msk2"), AF.Copy, scale=SP)
    for c in range(4):
        quant(V("b2%d" % c), V("b2s%d" % c), V("w2", 48 - 16 * c, 560 - 16 * c))
    keep(V("w3a"), V("ones", 0, 512), [[-16, 32], [0, 4], [128, 4]], A.is_ge, 0, 1)
    keep(V("w3"), V("w3a"), [[16, 32], [0, 4], [-128, 4]], A.is_ge, 15, -1)
    quant(V("b3"), V("b3s"), V("w3"))
    iota(V("im"), [[1, 16], [0, 4]], 0, 0)
    ts(V("maska"), V("im"), QC, None, A.is_equal)
    for i, val in enumerate((100.0, 3.0, 2.0, 1.0)):
        fill(V("thr", i, 128, 4), val)
    fill(V("d00"), 0.0)
    fill(V("d00", 3, 16, 4), 1.0)
    ts(V("lrep", 0, 1), ib(3), 3.0, None, A.add)
    fill(V("im", 0, 4), 0.0)
    ts(V("la4"), V("im", 0, 4), R4, None, A.add)
    fill(V("at", 0, 64), 0.0)
    fill(V("mt", 1536, 2048), 0.0)
    quant(V("mq", 384), V("mqs", 384), V("mt", 1536, 2048))
    ts(col(14), QC, 15.0, 2.0 ** -20 - 1.0, A.is_lt, A.mult)
    ts(THQ, col(14), 1.0, None, A.add)
    ts(V("t16"), V("t16"), 64.0, None, A.mult)
    tt(V("n16"), V("t16"), V("n16"), A.add)
    act(V("kb"), V("n16"), AF.Copy, lst=V("lq"))
    copy(V("lm"), V("mgw"))
    copy(V("mf"), V("mgw"))
    ts(V("jw"), V("iw"), 16.0, QC, A.mult, A.add)
    tt(V("mj"), V("mf"), V("jw"), A.subtract)
    ts(V("mj"), V("mj"), THQ, None, A.mult)
    ts(V("jw"), V("jw"), 0.25, None, A.add)

    def state(r, x, rows=(("up", "ups"),)):
        for i, (a, b) in enumerate(((0, CA), (CA, C))):
            quant(V("qc%d" % r, a, b), V("qs%d" % r, a, b), V(x, 4 * a, 4 * b))
            mm(V("pb%d" % i, 0, b - a), [(V(rows[0][0]), V(rows[0][1]), V("qc%d" % r, a, b), V("qs%d" % r, a, b))])

    for r in (1, 2, 3):
        x = ("xt", "x2", "x3")[r - 1]
        qc, qs, la, lp = V("qc%d" % r), V("qs%d" % r), V("la%d" % r), V("lp%d" % r)
        state(r, x)
        send(r, "c", V("rc%d" % r), qc, True, 6000.0)
        send(r, "s", V("rs%d" % r), qs, False, 4000.0)
        act(V("bw", 0, CA), V("pb0", 0, CA), AF.Sign)
        act(V("bw", CA, C), V("pb1", 0, C - CA), AF.Sign)
        for n in range(4):
            either(V("mt", n, 4 * C, 4), V("bw"), V("l%d" % n), relu=True)
        quant(V("mq", 0, C), V("mqs", 0, C), V("mt", 0, 4 * C))
        mm(V("pb6", 0, 128), [(V("mq", 128 * c, 128 * c + 128), V("mqs", 128 * c, 128 * c + 128), V("b2%d" % c), V("b2s%d" % c)) for c in range(4)])
        first = len(ops) - 1
        for k in range(7):
            sck = V("sc", 16 * k, 16 * k + 16)
            scan(sck, V("d0", 16 * k, 16 * k + 16) if k else V("d00"), V("pb6", 16 * k, 16 * k + 16))
            if k < 6:
                tt(V("d0", 16 * k + 16, 16 * k + 32), sck, V("thr", 0, 16), A.is_ge, lst=V("lrep", 0, 1))
            tt(V("at", 64 * k + 64, 64 * k + 128), sck, V("maska"), A.mult, lst=V("la4"))
        quant(V("aq"), V("aqs"), V("at"))
        mm(V("pb7", 0, 128), [(V("aq"), V("aqs"), V("b3"), V("b3s"))])
        tt(V("ph"), V("pb7", 0, 104), V("thr", 0, 104), A.is_ge)
        scan(V("sl"), V("ph"), V("cs%d" % r))
        copy(la, V("sl", 3, 104, 4))
        send(r, "l", lp, la, False, 2200.0)
        for b in range(4):
            mm(V("pb%d" % (2 + b), 0, C), [(V("e%d" % b), V("es%d" % b), qc, qs)], after=(first,))
            out_of_psum(V("fb%d" % b), V("pb%d" % (2 + b), 0, C))
        mm(V("pb0", 0, C), [(V("uc"), V("ucs"), qc, qs)])
        act(V("scw"), V("pb0", 0, C), AF.Sign)
        for b in range(4):
            mm(V("pb%d" % (2 + b), 0, C), [(V("e%d" % b), V("es%d" % b), V("rc%d" % r), V("rs%d" % r))])
            out_of_psum(V("fp%d" % b), V("pb%d" % (2 + b), 0, C))
        act(V("z"), V("scw"), AF.Relu, lst=la)
        ts(V("zz"), V("scw"), 0.0, None, A.max, lst=la)
        tt(V("nd"), V("z"), V("zz"), A.not_equal, lst=V("lm"))
        scan(V("ns"), V("kb"), V("nd"), f=0.5)
        tt(V("nm"), V("ns", 15, C, 16), V("mj"), A.mult)
        tt(V("tau"), V("nm"), V("jw"), A.add)
        copy(V("ltau"), V("tau"))
        act(V("p%d" % (r + 1)) if r < 3 else V("pl_t", C, 2 * C), V("p%d" % r), AF.Copy, lst=V("ltau"))
        if r == 3:
            iota(V("i520"), [[1, 520]], 0, 0)
            act(V("pl_t", 0, C), V("i520", 0, C), AF.Copy, lst=la)
            dma("S", [V("pl_t")], [], lambda: [(T.pl[:, :], T["pl_t"][0::16, :])])
        for a, e in ((0, CA), (CA, C)):
            for t in range(4):
                either(V("zt", 4 * a + t, 4 * e, 4), V("fp%d" % t), V("lp%d" % r, a // 16, e // 16))
            quant(V("zq", a, e), V("zqs", a, e), V("zt", 4 * a, 4 * e))
        for b in range(4):
            bias[0] = BIAS * (3 - b)
            for i, (a, e) in enumerate(((0, CA), (CA, C))):
                bank = V("pb%d" % ((2, 3, 4, 5, 0, 1, 6, 7)[4 * i + b]), 0, e - a)
                mm(bank, [(V("wq", 128 * b, 128 * b + 128), V("wqs", 128 * b, 128 * b + 128), V("zq", a, e), V("zqs", a, e))])
                out_of_psum(V("hs%d" % b, a, e), bank, scale=0.03125)
        nx = ("x2", "x3", "x4")[r - 1]
        for a, e in ((0, CA), (CA, C)):
            for b in range(4):
                bias[0] = BIAS * (3 - b)
                tt(V(nx, 4 * a + b, 4 * e, 4), V("hs%d" % b), V("fb%d" % b, a, e), A.add, lst=V("la%d" % r, a // 16, e // 16))
        bias[0] = 0.0
        if r < 3:
            powers(r + 1)
    quant(V("vq"), V("vqs"), V("vt"))
    for i, (a, b) in enumerate(((0, CA), (CA, C))):
        quant(V("qc4", a, b), V("qs4", a, b), V("x4", 4 * a, 4 * b))
        dma("S", [V("qc4", a, b)], [], lambda a=a, b=b: [(T.oc[:, 4 * a:4 * b], T["qc4"][:, a:b].bitcast(dt.uint8))])
        mm(V("pb%d" % i, 0, b - a), [(V("vq"), V("vqs"), V("qc4", a, b), V("qs4", a, b))])
        out_of_psum(V("yt", a, b), V("pb%d" % i, 0, b - a))
        dma("S", [V("yt", a, b)], [], lambda a=a, b=b: [(T.y[:, a:b], T["yt"][:, a:b])])
    dma("S", [V("qs4")], [], lambda: [(T.osc[4 * k:4 * k + 4, :], T["qs4"][32 * k:32 * k + 4, :]) for k in range(4)])

    n = len(ops)
    users = [[] for _ in range(n)]
    for i, o in enumerate(ops):
        for j in o["deps"]:
            users[j].append(i)
    prio = [0.0] * n
    for i in range(n - 1, -1, -1):
        prio[i] = ops[i]["cost"] + max([prio[u] + WAKE for u in users[i]] + [0.0])
    prio = [p + o["bias"] for p, o in zip(prio, ops)]
    free = {k: 0.0 for k in "VAPGSR"}
    end = [None] * n
    left = [len(o["deps"]) for o in ops]
    ready = [i for i in range(n) if not left[i]]
    order = []
    while ready:
        best = None
        cand = []
        for i in ready:
            o = ops[i]
            at = max([end[j] + WAKE for j in o["deps"]] + [0.0])
            if o["kind"] == "r":
                at = end[list(o["deps"])[0]] if len(o["deps"]) == 1 else max(end[j] for j in o["deps"])
                cand.append((at, i, "R"))
                continue
            for q in o["q"]:
                cand.append((max(at, free[q]), i, q))
        first = min(c[0] for c in cand)
        best = max((c for c in cand if c[0] <= first + 20.0), key=lambda c: (prio[c[1]], -c[0]))
        late = best[0] + ops[best[1]]["cost"]
        soon = [c for c in cand if c[2] == best[2] and prio[c[1]] > prio[best[1]] and c[0] - best[0] < LOOK * (late - c[0])]
        if soon:
            best = max(soon, key=lambda c: (prio[c[1]], -c[0]))
        at, i, q = best
        o = ops[i]
        if o["kind"] == "d":
            free[q] = at + 60.0 * (o["amount"] // 16)
            end[i] = free[q] + o["cost"]
        elif o["kind"] == "r":
            end[i] = at + o["cost"]
        else:
            free[q] = end[i] = at + o["cost"]
        order.append((i, q, at))
        ready.remove(i)
        for u in users[i]:
            left[u] -= 1
            if not left[u]:
                ready.append(u)

    eng = {"V": g.vector, "A": g.scalar, "P": g.tensor, "G": g, "S": g.sync}
    csem = {"V": "s_v", "A": "s_a", "P": "s_p", "G": "s_g"}
    count = {k: 0 for k in csem}
    known = {k: {} for k in "VAPGS"}
    token, clock, qof = [None] * n, [None] * n, [None] * n
    for i, q, at in order:
        o = ops[i]
        qof[i] = q
        if o["kind"] == "r":
            token[i], clock[i] = (o["sem"], o["amount"]), {o["sem"]: o["amount"]}
            for j in o["deps"]:
                for s, v in (clock[j] or {}).items():
                    clock[i][s] = max(clock[i].get(s, 0), 0)
            continue
        e = eng[q]
        need = []
        for j, raw in o["deps"].items():
            if token[j] is None:
                continue
            need.append(j)
        need.sort(key=lambda j: -end[j])
        for j in need:
            s, v = token[j]
            if known[q].get(s, 0) >= v:
                continue
            e.wait_ge(T.sem[s], v)
            for s2, v2 in clock[j].items():
                known[q][s2] = max(known[q].get(s2, 0), v2)
        call = o["emit"](e, q) if len(o["q"]) > 1 else o["emit"](e)
        if o["kind"] == "c":
            count[q] += 1
            call.then_inc(T.sem[csem[q]], 1)
            token[i] = (csem[q], count[q])
        elif o["kind"] == "d":
            token[i] = (o["sem"], o["amount"])
        if token[i]:
            clock[i] = dict(known[q])
            clock[i][token[i][0]] = max(clock[i].get(token[i][0], 0), token[i][1])
    for q in csem:
        g.wait_ge(T.sem[csem[q]], count[q])
    for o in ops:
        if o["kind"] in "dr":
            g.wait_ge(T.sem[o["sem"]], o["amount"])
    g.wait_ge(T.sem["loc"], sent[0])
